import numpy as np
import ml_dtypes


def mxq(x, axis, fmt="e4m3"):
    dtype, down = {"e4m3": (ml_dtypes.float8_e4m3fn, 7), "e5m2": (ml_dtypes.float8_e5m2, 14)}[fmt]
    v = np.moveaxis(np.asarray(x, np.float32).astype(ml_dtypes.bfloat16).astype(np.float64), axis, -1)
    blocks = v.reshape(v.shape[:-1] + (-1, 32))
    amax = np.abs(blocks).max(-1, keepdims=True)
    byte = np.maximum(np.where(amax > 0, np.frexp(amax)[1] - 1 + 127, 0) - down, 1)
    scale = np.exp2(byte - 127.0)
    codes = (blocks / scale).astype(np.float32).astype(dtype).astype(np.float64)
    return np.moveaxis((codes * scale).reshape(v.shape), -1, axis)


WIDE = False


def mx_kscale(k):
    if not WIDE:
        return np.ones(k)
    levels = np.array([30, -30])
    if k % 512:
        return np.exp2(np.random.permutation(np.resize(levels, k // 32))).repeat(32)
    a = np.empty((k // 512, 16))
    for p in range(k // 512):
        a[p, :8] = np.random.permutation(np.resize(levels, 8))
        for g in range(8):
            far = levels[np.abs(levels - a[p, g]) >= 10]
            a[p, g + 8] = far[np.random.randint(len(far))]
    return np.exp2(a.ravel()).repeat(32)


def f64(x):
    return np.asarray(x).astype(np.float64)


def striped(idx):
    return np.tile(np.asarray(idx).reshape(-1, 16).T, (8, 1)).astype(np.uint16)


def unstriped(offs):
    return offs[:16].T.reshape(-1).astype(np.int64)


E2M1 = np.array([0.0, 0.5, 1.0, 1.5, 2.0, 3.0, 4.0, 6.0, -0.0, -0.5, -1.0, -1.5, -2.0, -3.0, -4.0, -6.0])


def pack_weight(w, fmt):
    k, n = w.shape
    w = f64(np.asarray(w, np.float32).astype(ml_dtypes.bfloat16)).reshape(k // 32, 32, n)
    amax = np.abs(w).max(1)
    if fmt in ("e4m3", "e5m2"):
        byte = np.frexp(amax)[1] - 1 + 127 - (7 if fmt == "e4m3" else 14)
    else:
        mant, ex = np.frexp(amax / 6.0)
        byte = np.where(mant > 0.5, ex, ex - 1) + 127
    byte = np.clip(np.where(amax > 0, byte, 1), 1, 254)
    scaled = (w * np.exp2(127.0 - byte)[:, None, :]).reshape(k, n).astype(np.float32)
    by_word = np.ascontiguousarray(scaled.reshape(k // 512, 128, 4, n).transpose(0, 1, 3, 2))
    if fmt in ("e4m3", "e5m2"):
        words = by_word.astype(ml_dtypes.float8_e4m3fn if fmt == "e4m3" else ml_dtypes.float8_e5m2).view(np.uint8)
    else:
        c = by_word.astype(ml_dtypes.float4_e2m1fn).view(np.uint8) & 0xF
        words = (c[..., 0::2] | (c[..., 1::2] << 4)).reshape(k // 512, 128, 2 * n)
    return np.ascontiguousarray(words), np.ascontiguousarray(byte.astype(np.uint8).reshape(k // 512, 16, n))


def unpack_weight(words, scales, fmt):
    g, _, n = scales.shape
    words = np.ascontiguousarray(words).reshape(g, 128, n, -1)
    if fmt in ("e4m3", "e5m2"):
        vals = words.view(ml_dtypes.float8_e4m3fn if fmt == "e4m3" else ml_dtypes.float8_e5m2).astype(np.float64)
    else:
        nib = np.empty((g, 128, n, 4), np.uint8)
        nib[..., 0::2] = words & 0xF
        nib[..., 1::2] = words >> 4
        vals = E2M1[nib]
    vals = vals * np.repeat(np.exp2(scales.astype(np.float64) - 127.0), 8, axis=1)[..., None]
    return vals.transpose(0, 1, 3, 2).reshape(g * 512, n)


K, T, J, N, L = 1024, 1024, 256, 256, 512


def setup_inputs():
    n = np.random.standard_normal
    idx = np.random.permutation(T)[:J]
    fk = mx_kscale(K)
    fl = mx_kscale(L)
    xtp = pack_weight(n((K, T)) * np.random.uniform(0.4, 1.6, (1, T)) / fk[:, None], "e5m2")
    wap = pack_weight(n((K, N)) * 1 / np.sqrt(K) * fk[:, None], "e2m1")
    wbp = pack_weight(n((L, N)) * 1 / np.sqrt(L) * fl[:, None], "e2m1")
    return {
        "xt_words": xtp[0],
        "xt_scales": xtp[1],
        "wa_words": wap[0],
        "wa_scales": wap[1],
        "sx": (n((L, J)) * np.random.uniform(0.4, 1.6, (1, J)) / fl[:, None]).astype(np.float32),
        "wb_words": wbp[0],
        "wb_scales": wbp[1],
        "bi": (np.random.uniform(-0.6, 0.6, (1, N))).astype(np.float32),
        "offs": striped(idx),
    }


def reference(xt_words, xt_scales, wa_words, wa_scales, sx, wb_words, wb_scales, bi, offs):
    idx = unstriped(offs)
    xtu = unpack_weight(xt_words, xt_scales, "e5m2")
    wau = unpack_weight(wa_words, wa_scales, "e2m1")
    wbu = unpack_weight(wb_words, wb_scales, "e2m1")
    xtidxg = xtu[:, idx]
    a = xtidxg.T @ wau
    sxq = mxq(f64(sx), 0, "e5m2")
    b0 = sxq.T @ wbu
    b2 = b0 + f64(bi)
    e = np.exp(0.6 * (a - b2))
    y = 256.0 * e / np.sum(e, axis=1, keepdims=True)
    return y

@@ -1,0 +1,156 @@
+from contextlib import ExitStack
+
+import concourse.mybir as mybir
+from concourse.masks import make_identity
+
+K, T, J, N, L = 1024, 1024, 256, 256, 512
+FLOPS = 2 * J * N * (K + L)
+
+F32 = mybir.dt.float32
+BF16 = mybir.dt.bfloat16
+I32 = mybir.dt.int32
+U32 = mybir.dt.uint32
+U16 = mybir.dt.uint16
+U8 = mybir.dt.uint8
+E5M2X4 = mybir.dt.float8_e5m2_x4
+E2M1X4 = mybir.dt.float4_e2m1fn_x4
+ALU = mybir.AluOpType
+ACT = mybir.ActivationFunctionType
+
+P = 128
+PASSES = K // 512
+HALVES = J // P
+GAP = 0.6
+TOTAL = 256.0
+
+
+def tile_list_rows_owninput_sharesofgap_kernel(
+    tc, xt_words, xt_scales, wa_words, wa_scales, sx, wb_words, wb_scales, bi, offs, out
+):
+    nc = tc.nc
+    with ExitStack() as ctx:
+        pool = ctx.enter_context(tc.tile_pool(name="keep", bufs=1))
+        psum = ctx.enter_context(tc.psum_pool(name="psum", bufs=1))
+
+        offsets = pool.tile([P, J // 16], U16, name="offsets")
+        x_words = [pool.tile([P, T], U32, name=f"x_words{z}", align_bytes=64) for z in range(PASSES)]
+        x_scales = pool.tile([P, PASSES * T], U8, name="x_scales", align_bytes=64)
+        w_scales = pool.tile([P, (PASSES + 1) * N], U8, name="w_scales", align_bytes=64)
+        wa_codes = pool.tile([P, PASSES * 2 * N], U8, name="wa_codes", align_bytes=64)
+        wb_codes = pool.tile([P, 2 * N], U8, name="wb_codes", align_bytes=64)
+        sx_raw = pool.tile([P, 4, J], F32, name="sx_raw")
+        bias_col = pool.tile([P, 2], F32, name="bias_col")
+        ident = pool.tile([P, P], F32, name="ident")
+
+        nc.vector.memset(x_scales[:].bitcast(I32), 0)
+        nc.vector.memset(w_scales[:].bitcast(I32), 0)
+        nc.vector.memset(ident[:], 0.0)
+
+        def load_words(z):
+            nc.sync.dma_start(
+                out=x_words[z][:].bitcast(I32),
+                in_=xt_words[z].rearrange("p c r -> p (c r)").bitcast(I32),
+            )
+
+        def load_scale_rows(queue, plane, rows, q):
+            queue.dma_start(
+                out=plane[32 * q : 32 * q + 4, :].bitcast(I32).rearrange("r (z c) -> r z c", z=rows.shape[0]),
+                in_=rows[:, 4 * q : 4 * q + 4, :].rearrange("z r c -> r z c").bitcast(I32),
+            )
+
+        nc.sync.dma_start(offsets[:], offs)
+        load_words(0)
+        nc.sync.dma_start(out=bias_col[:], in_=bi.rearrange("o (p c) -> (o p) c", c=2))
+        for q in range(4):
+            load_scale_rows(nc.sync, x_scales, xt_scales, q)
+        nc.sync.dma_start(out=sx_raw[:], in_=sx.rearrange("(p t) j -> p t j", t=4))
+        load_words(1)
+        nc.gpsimd.dma_start(
+            out=wa_codes[:].bitcast(I32).rearrange("p (z b) -> p z b", z=PASSES),
+            in_=wa_words.rearrange("z p b -> p z b").bitcast(I32),
+        )
+        make_identity(nc, ident[:], nomemset=True)
+        nc.gpsimd.dma_start(out=wb_codes[:].bitcast(I32), in_=wb_words[0].bitcast(I32))
+        load_scale_rows(nc.gpsimd, w_scales[:, PASSES * N :], wb_scales, 3)
+        for q in range(4):
+            load_scale_rows(nc.sync, w_scales[:, : PASSES * N], wa_scales, q)
+        for q in range(3):
+            load_scale_rows(nc.sync, w_scales[:, PASSES * N :], wb_scales, q)
+
+        g_words = [pool.tile([P, J], U32, name=f"g_words{z}", align_bytes=64) for z in range(PASSES)]
+        g_scales = [pool.tile([P, J], U8, name=f"g_scales{z}", align_bytes=64) for z in range(PASSES)]
+        nc.vector.tensor_copy(g_words[0][:], x_words[0][:].indirect(offsets[:]))
+        for z in range(PASSES):
+            nc.vector.tensor_copy(g_scales[z][:], x_scales[:, z * T : (z + 1) * T].indirect(offsets[:]))
+
+        grouped = pool.tile([P, J, 4], BF16, name="grouped", align_bytes=64)
+        nc.scalar.activation(
+            out=grouped[:].rearrange("p (c i) t -> p c t i", i=4),
+            in_=sx_raw[:].rearrange("p t (c i) -> p c t i", i=4),
+            func=ACT.Copy,
+            scale=-1.0,
+        )
+        s_words = pool.tile([P, J], U32, name="s_words", align_bytes=64)
+        s_scales = pool.tile([P, J], U8, name="s_scales", align_bytes=64)
+        nc.vector.quantize_mx(
+            out=s_words[:].bitcast(E5M2X4),
+            scales=s_scales[:],
+            in_=grouped[:].rearrange("p j t -> p (j t)"),
+        )
+
+        bias_bank = psum.tile([P, 2, P], F32, name="bias_bank")
+        for c in range(2):
+            nc.tensor.transpose(bias_bank[:, c, :], bias_col[:, c : c + 1].to_broadcast([P, P]), ident[:])
+        bias_rows = pool.tile([P, N], F32, name="bias_rows")
+        nc.scalar.activation(
+            out=bias_rows[:].rearrange("m (p c) -> m p c", c=2),
+            in_=bias_bank[:].rearrange("m c p -> m p c"),
+            func=ACT.Copy,
+            scale=GAP,
+        )
+
+        for h in range(HALVES):
+            slots = slice(h * P, (h + 1) * P)
+            nc.vector.tensor_copy(
+                g_words[1][:, slots], x_words[1][:].indirect(offsets[:, h * 8 : (h + 1) * 8])
+            )
+
+        banks = [psum.tile([P, N], F32, name=f"gap{h}") for h in range(HALVES)]
+        for h in range(HALVES):
+            slots = slice(h * P, (h + 1) * P)
+            operands = [
+                (g_words[0], g_scales[0], wa_codes[:, : 2 * N], w_scales[:, :N]),
+                (s_words, s_scales, wb_codes[:], w_scales[:, 2 * N :]),
+                (g_words[1], g_scales[1], wa_codes[:, 2 * N :], w_scales[:, N : 2 * N]),
+            ]
+            for i, (words, scales, w_codes, w_plane) in enumerate(operands):
+                nc.tensor.matmul_mx(
+                    out=banks[h][:],
+                    lhsT=words[:, slots].bitcast(E5M2X4),
+                    lhsT_scale=scales[:, slots],
+                    rhs=w_codes.bitcast(E2M1X4),
+                    rhs_scale=w_plane,
+                    start=(i == 0),
+                    stop=(i == len(operands) - 1),
+                )
+
+        for h in range(HALVES):
+            slots = slice(h * P, (h + 1) * P)
+            neg_gap = pool.tile([P, N], F32, name=f"neg_gap{h}")
+            nc.vector.scalar_tensor_tensor(
+                out=neg_gap[:], in0=banks[h][:], scalar=-GAP, in1=bias_rows[:], op0=ALU.mult, op1=ALU.add
+            )
+            least = pool.tile([P, 1], F32, name=f"least{h}")
+            nc.vector.tensor_reduce(out=least[:], in_=neg_gap[:], axis=mybir.AxisListType.X, op=ALU.min)
+            e = pool.tile([P, N], F32, name=f"e{h}")
+            total = pool.tile([P, 1], F32, name=f"total{h}")
+            nc.scalar.activation(
+                out=e[:], in_=neg_gap[:], func=ACT.Exp, bias=least[:], scale=-1.0, accum_out=total[:]
+            )
+            inverse = pool.tile([P, 1], F32, name=f"inverse{h}")
+            nc.vector.reciprocal(inverse[:], total[:])
+            shares = pool.tile([P, N], F32, name=f"shares{h}")
+            nc.vector.tensor_scalar(
+                out=shares[:], in0=e[:], scalar1=inverse[:], scalar2=TOTAL, op0=ALU.mult, op1=ALU.mult
+            )
+            nc.sync.dma_start(out=out[slots, :], in_=shares[:])

@@ -33,9 +33,10 @@ def tile_list_rows_owninput_sharesofgap_kernel(
         psum = ctx.enter_context(tc.psum_pool(name="psum", bufs=1))
 
         offsets = pool.tile([P, J // 16], U16, name="offsets")
-        x_words = [pool.tile([P, T], U32, name=f"x_words{z}", align_bytes=64) for z in range(PASSES)]
+        x_words = [pool.tile([P, T], U32, name=f"x_words{z}", tag=f"x_words{z}", align_bytes=64) for z in range(PASSES)]
         x_scales = pool.tile([P, PASSES * T], U8, name="x_scales", align_bytes=64)
-        w_scales = pool.tile([P, (PASSES + 1) * N], U8, name="w_scales", align_bytes=64)
+        wa_plane = pool.tile([P, PASSES * N], U8, name="wa_plane", align_bytes=64)
+        wb_plane = pool.tile([P, N], U8, name="wb_plane", align_bytes=64)
         wa_codes = pool.tile([P, PASSES * 2 * N], U8, name="wa_codes", align_bytes=64)
         wb_codes = pool.tile([P, 2 * N], U8, name="wb_codes", align_bytes=64)
         sx_raw = pool.tile([P, 4, J], F32, name="sx_raw")
@@ -43,8 +44,9 @@ def tile_list_rows_owninput_sharesofgap_kernel(
         ident = pool.tile([P, P], F32, name="ident")
 
         nc.vector.memset(x_scales[:].bitcast(I32), 0)
-        nc.vector.memset(w_scales[:].bitcast(I32), 0)
+        nc.vector.memset(wa_plane[:].bitcast(I32), 0)
         nc.vector.memset(ident[:], 0.0)
+        nc.vector.memset(wb_plane[:].bitcast(I32), 0)
 
         def load_words(z):
             nc.sync.dma_start(
@@ -52,34 +54,32 @@ def tile_list_rows_owninput_sharesofgap_kernel(
                 in_=xt_words[z].rearrange("p c r -> p (c r)").bitcast(I32),
             )
 
-        def load_scale_rows(queue, plane, rows, q):
+        def load_scale_rows(queue, plane, rows, r):
             queue.dma_start(
-                out=plane[32 * q : 32 * q + 4, :].bitcast(I32).rearrange("r (z c) -> r z c", z=rows.shape[0]),
-                in_=rows[:, 4 * q : 4 * q + 4, :].rearrange("z r c -> r z c").bitcast(I32),
+                out=plane[r:P:32, :].bitcast(I32).rearrange("q (z c) -> q z c", z=rows.shape[0]),
+                in_=rows[:, r:16:4, :].rearrange("z q c -> q z c").bitcast(I32),
             )
 
         nc.sync.dma_start(offsets[:], offs)
-        load_words(0)
+        nc.scalar.dma_start(out=sx_raw[:], in_=sx.rearrange("(p t) j -> p t j", t=4))
         nc.sync.dma_start(out=bias_col[:], in_=bi.rearrange("o (p c) -> (o p) c", c=2))
-        for q in range(4):
-            load_scale_rows(nc.sync, x_scales, xt_scales, q)
-        nc.sync.dma_start(out=sx_raw[:], in_=sx.rearrange("(p t) j -> p t j", t=4))
-        load_words(1)
         nc.gpsimd.dma_start(
             out=wa_codes[:].bitcast(I32).rearrange("p (z b) -> p z b", z=PASSES),
             in_=wa_words.rearrange("z p b -> p z b").bitcast(I32),
         )
         make_identity(nc, ident[:], nomemset=True)
-        nc.gpsimd.dma_start(out=wb_codes[:].bitcast(I32), in_=wb_words[0].bitcast(I32))
-        load_scale_rows(nc.gpsimd, w_scales[:, PASSES * N :], wb_scales, 3)
-        for q in range(4):
-            load_scale_rows(nc.sync, w_scales[:, : PASSES * N], wa_scales, q)
-        for q in range(3):
-            load_scale_rows(nc.sync, w_scales[:, PASSES * N :], wb_scales, q)
+        for r in range(4):
+            load_scale_rows(nc.sync, x_scales, xt_scales, r)
+        load_words(0)
+        for r in range(4):
+            load_scale_rows(nc.sync, wa_plane, wa_scales, r)
+        load_words(1)
+        nc.sync.dma_start(out=wb_codes[:].bitcast(I32), in_=wb_words[0].bitcast(I32))
+        for r in range(4):
+            load_scale_rows(nc.sync, wb_plane, wb_scales, r)
 
         g_words = [pool.tile([P, J], U32, name=f"g_words{z}", align_bytes=64) for z in range(PASSES)]
         g_scales = [pool.tile([P, J], U8, name=f"g_scales{z}", align_bytes=64) for z in range(PASSES)]
-        nc.vector.tensor_copy(g_words[0][:], x_words[0][:].indirect(offsets[:]))
         for z in range(PASSES):
             nc.vector.tensor_copy(g_scales[z][:], x_scales[:, z * T : (z + 1) * T].indirect(offsets[:]))
 
@@ -90,13 +90,15 @@ def tile_list_rows_owninput_sharesofgap_kernel(
             func=ACT.Copy,
             scale=-1.0,
         )
-        s_words = pool.tile([P, J], U32, name="s_words", align_bytes=64)
+        s_words = pool.tile([P, J], U32, name="s_words", tag="x_words0", align_bytes=64)
         s_scales = pool.tile([P, J], U8, name="s_scales", align_bytes=64)
         nc.vector.quantize_mx(
             out=s_words[:].bitcast(E5M2X4),
             scales=s_scales[:],
             in_=grouped[:].rearrange("p j t -> p (j t)"),
         )
+
+        nc.vector.tensor_copy(g_words[0][:], x_words[0][:].indirect(offsets[:]))
 
         bias_bank = psum.tile([P, 2, P], F32, name="bias_bank")
         for c in range(2):
@@ -119,9 +121,9 @@ def tile_list_rows_owninput_sharesofgap_kernel(
         for h in range(HALVES):
             slots = slice(h * P, (h + 1) * P)
             operands = [
-                (g_words[0], g_scales[0], wa_codes[:, : 2 * N], w_scales[:, :N]),
-                (s_words, s_scales, wb_codes[:], w_scales[:, 2 * N :]),
-                (g_words[1], g_scales[1], wa_codes[:, 2 * N :], w_scales[:, N : 2 * N]),
+                (g_words[0], g_scales[0], wa_codes[:, : 2 * N], wa_plane[:, :N]),
+                (s_words, s_scales, wb_codes[:], wb_plane[:]),
+                (g_words[1], g_scales[1], wa_codes[:, 2 * N :], wa_plane[:, N:]),
             ]
             for i, (words, scales, w_codes, w_plane) in enumerate(operands):
                 nc.tensor.matmul_mx(

@@ -68,13 +68,13 @@ def tile_list_rows_owninput_sharesofgap_kernel(
             in_=wa_words.rearrange("z p b -> p z b").bitcast(I32),
         )
         make_identity(nc, ident[:], nomemset=True)
+        nc.gpsimd.dma_start(out=wb_codes[:].bitcast(I32), in_=wb_words[0].bitcast(I32))
         for r in range(4):
             load_scale_rows(nc.sync, x_scales, xt_scales, r)
         load_words(0)
         for r in range(4):
             load_scale_rows(nc.sync, wa_plane, wa_scales, r)
         load_words(1)
-        nc.sync.dma_start(out=wb_codes[:].bitcast(I32), in_=wb_words[0].bitcast(I32))
         for r in range(4):
             load_scale_rows(nc.sync, wb_plane, wb_scales, r)
 
@@ -90,6 +90,7 @@ def tile_list_rows_owninput_sharesofgap_kernel(
             func=ACT.Copy,
             scale=-1.0,
         )
+        nc.vector.tensor_copy(g_words[0][:], x_words[0][:].indirect(offsets[:]))
         s_words = pool.tile([P, J], U32, name="s_words", tag="x_words0", align_bytes=64)
         s_scales = pool.tile([P, J], U8, name="s_scales", align_bytes=64)
         nc.vector.quantize_mx(
@@ -97,8 +98,6 @@ def tile_list_rows_owninput_sharesofgap_kernel(
             scales=s_scales[:],
             in_=grouped[:].rearrange("p j t -> p (j t)"),
         )
-
-        nc.vector.tensor_copy(g_words[0][:], x_words[0][:].indirect(offsets[:]))
 
         bias_bank = psum.tile([P, 2, P], F32, name="bias_bank")
         for c in range(2):

from contextlib import ExitStack

import concourse.mybir as mybir
from concourse.masks import make_identity

K, T, J, N, L = 1024, 1024, 256, 256, 512
FLOPS = 2 * J * N * (K + L)

F32 = mybir.dt.float32
BF16 = mybir.dt.bfloat16
I32 = mybir.dt.int32
U32 = mybir.dt.uint32
U16 = mybir.dt.uint16
U8 = mybir.dt.uint8
E5M2X4 = mybir.dt.float8_e5m2_x4
E2M1X4 = mybir.dt.float4_e2m1fn_x4
ALU = mybir.AluOpType
ACT = mybir.ActivationFunctionType

P = 128
PASSES = K // 512
HALVES = J // P
GAP = 0.6
TOTAL = 256.0


def tile_list_rows_owninput_sharesofgap_kernel(
    tc, xt_words, xt_scales, wa_words, wa_scales, sx, wb_words, wb_scales, bi, offs, out
):
    nc = tc.nc
    with ExitStack() as ctx:
        pool = ctx.enter_context(tc.tile_pool(name="keep", bufs=1))
        psum = ctx.enter_context(tc.psum_pool(name="psum", bufs=1))

        offsets = pool.tile([P, J // 16], U16, name="offsets")
        x_words = [pool.tile([P, T], U32, name=f"x_words{z}", tag=f"x_words{z}", align_bytes=64) for z in range(PASSES)]
        x_scales = pool.tile([P, PASSES * T], U8, name="x_scales", align_bytes=64)
        wa_plane = pool.tile([P, PASSES * N], U8, name="wa_plane", align_bytes=64)
        wb_plane = pool.tile([P, N], U8, name="wb_plane", align_bytes=64)
        wa_codes = pool.tile([P, PASSES * 2 * N], U8, name="wa_codes", align_bytes=64)
        wb_codes = pool.tile([P, 2 * N], U8, name="wb_codes", align_bytes=64)
        sx_raw = pool.tile([P, 4, J], F32, name="sx_raw")
        bias_col = pool.tile([P, 2], F32, name="bias_col")
        ident = pool.tile([P, P], F32, name="ident")

        nc.vector.memset(x_scales[:].bitcast(I32), 0)
        nc.vector.memset(wa_plane[:].bitcast(I32), 0)
        nc.vector.memset(ident[:], 0.0)
        nc.vector.memset(wb_plane[:].bitcast(I32), 0)

        def load_words(z):
            nc.sync.dma_start(
                out=x_words[z][:].bitcast(I32),
                in_=xt_words[z].rearrange("p c r -> p (c r)").bitcast(I32),
            )

        def load_scale_rows(queue, plane, rows, r):
            queue.dma_start(
                out=plane[r:P:32, :].bitcast(I32).rearrange("q (z c) -> q z c", z=rows.shape[0]),
                in_=rows[:, r:16:4, :].rearrange("z q c -> q z c").bitcast(I32),
            )

        nc.sync.dma_start(offsets[:], offs)
        nc.scalar.dma_start(out=sx_raw[:], in_=sx.rearrange("(p t) j -> p t j", t=4))
        nc.sync.dma_start(out=bias_col[:], in_=bi.rearrange("o (p c) -> (o p) c", c=2))
        nc.gpsimd.dma_start(
            out=wa_codes[:].bitcast(I32).rearrange("p (z b) -> p z b", z=PASSES),
            in_=wa_words.rearrange("z p b -> p z b").bitcast(I32),
        )
        make_identity(nc, ident[:], nomemset=True)
        nc.gpsimd.dma_start(out=wb_codes[:].bitcast(I32), in_=wb_words[0].bitcast(I32))
        for r in range(4):
            load_scale_rows(nc.sync, x_scales, xt_scales, r)
        load_words(0)
        for r in range(4):
            load_scale_rows(nc.sync, wa_plane, wa_scales, r)
        load_words(1)
        for r in range(4):
            load_scale_rows(nc.sync, wb_plane, wb_scales, r)

        g_words = [pool.tile([P, J], U32, name=f"g_words{z}", align_bytes=64) for z in range(PASSES)]
        g_scales = [pool.tile([P, J], U8, name=f"g_scales{z}", align_bytes=64) for z in range(PASSES)]
        for z in range(PASSES):
            nc.vector.tensor_copy(g_scales[z][:], x_scales[:, z * T : (z + 1) * T].indirect(offsets[:]))

        grouped = pool.tile([P, J, 4], BF16, name="grouped", align_bytes=64)
        nc.scalar.activation(
            out=grouped[:].rearrange("p (c i) t -> p c t i", i=4),
            in_=sx_raw[:].rearrange("p t (c i) -> p c t i", i=4),
            func=ACT.Copy,
            scale=-1.0,
        )
        nc.vector.tensor_copy(g_words[0][:], x_words[0][:].indirect(offsets[:]))
        s_words = pool.tile([P, J], U32, name="s_words", tag="x_words0", align_bytes=64)
        s_scales = pool.tile([P, J], U8, name="s_scales", align_bytes=64)
        nc.vector.quantize_mx(
            out=s_words[:].bitcast(E5M2X4),
            scales=s_scales[:],
            in_=grouped[:].rearrange("p j t -> p (j t)"),
        )

        bias_bank = psum.tile([P, 2, P], F32, name="bias_bank")
        for c in range(2):
            nc.tensor.transpose(bias_bank[:, c, :], bias_col[:, c : c + 1].to_broadcast([P, P]), ident[:])
        bias_rows = pool.tile([P, N], F32, name="bias_rows")
        nc.scalar.activation(
            out=bias_rows[:].rearrange("m (p c) -> m p c", c=2),
            in_=bias_bank[:].rearrange("m c p -> m p c"),
            func=ACT.Copy,
            scale=GAP,
        )

        for h in range(HALVES):
            slots = slice(h * P, (h + 1) * P)
            nc.vector.tensor_copy(
                g_words[1][:, slots], x_words[1][:].indirect(offsets[:, h * 8 : (h + 1) * 8])
            )

        banks = [psum.tile([P, N], F32, name=f"gap{h}") for h in range(HALVES)]
        for h in range(HALVES):
            slots = slice(h * P, (h + 1) * P)
            operands = [
                (g_words[0], g_scales[0], wa_codes[:, : 2 * N], wa_plane[:, :N]),
                (s_words, s_scales, wb_codes[:], wb_plane[:]),
                (g_words[1], g_scales[1], wa_codes[:, 2 * N :], wa_plane[:, N:]),
            ]
            for i, (words, scales, w_codes, w_plane) in enumerate(operands):
                nc.tensor.matmul_mx(
                    out=banks[h][:],
                    lhsT=words[:, slots].bitcast(E5M2X4),
                    lhsT_scale=scales[:, slots],
                    rhs=w_codes.bitcast(E2M1X4),
                    rhs_scale=w_plane,
                    start=(i == 0),
                    stop=(i == len(operands) - 1),
                )

        for h in range(HALVES):
            slots = slice(h * P, (h + 1) * P)
            neg_gap = pool.tile([P, N], F32, name=f"neg_gap{h}")
            nc.vector.scalar_tensor_tensor(
                out=neg_gap[:], in0=banks[h][:], scalar=-GAP, in1=bias_rows[:], op0=ALU.mult, op1=ALU.add
            )
            least = pool.tile([P, 1], F32, name=f"least{h}")
            nc.vector.tensor_reduce(out=least[:], in_=neg_gap[:], axis=mybir.AxisListType.X, op=ALU.min)
            e = pool.tile([P, N], F32, name=f"e{h}")
            total = pool.tile([P, 1], F32, name=f"total{h}")
            nc.scalar.activation(
                out=e[:], in_=neg_gap[:], func=ACT.Exp, bias=least[:], scale=-1.0, accum_out=total[:]
            )
            inverse = pool.tile([P, 1], F32, name=f"inverse{h}")
            nc.vector.reciprocal(inverse[:], total[:])
            shares = pool.tile([P, N], F32, name=f"shares{h}")
            nc.vector.tensor_scalar(
                out=shares[:], in0=e[:], scalar1=inverse[:], scalar2=TOTAL, op0=ALU.mult, op1=ALU.mult
            )
            nc.sync.dma_start(out=out[slots, :], in_=shares[:])
